import numpy as np
import ml_dtypes


def mxq(x, axis, fmt="e4m3"):
    dtype, down = {"e4m3": (ml_dtypes.float8_e4m3fn, 7), "e5m2": (ml_dtypes.float8_e5m2, 14)}[fmt]
    v = np.moveaxis(np.asarray(x, np.float32).astype(ml_dtypes.bfloat16).astype(np.float64), axis, -1)
    blocks = v.reshape(v.shape[:-1] + (-1, 32))
    amax = np.abs(blocks).max(-1, keepdims=True)
    byte = np.maximum(np.where(amax > 0, np.frexp(amax)[1] - 1 + 127, 0) - down, 1)
    scale = np.exp2(byte - 127.0)
    codes = (blocks / scale).astype(np.float32).astype(dtype).astype(np.float64)
    return np.moveaxis((codes * scale).reshape(v.shape), -1, axis)


WIDE = False


def mx_kscale(k):
    if not WIDE:
        return np.ones(k)
    levels = np.array([10, -10, 5, -5, 0])
    if k % 512:
        return np.exp2(np.random.permutation(np.resize(levels, k // 32))).repeat(32)
    a = np.empty((k // 512, 16))
    for p in range(k // 512):
        a[p, :8] = np.random.permutation(np.resize(levels, 8))
        for g in range(8):
            far = levels[np.abs(levels - a[p, g]) >= 10]
            a[p, g + 8] = far[np.random.randint(len(far))]
    return np.exp2(a.ravel()).repeat(32)


def f64(x):
    return np.asarray(x).astype(np.float64)


def striped(idx):
    return np.tile(idx.reshape(-1, 16).T, (8, 1)).astype(np.uint16)


def unstriped(offs):
    return offs[:16].T.reshape(-1).astype(np.int64)


def striped8(idx):
    return np.concatenate([x.reshape(-1, 16).T for x in idx]).astype(np.uint16)


def runs(offs, k):
    lists = np.stack([offs[16 * r : 16 * r + 16].T.reshape(-1) for r in range(8)]).astype(np.int64)
    return lists[np.arange(k) % 512 // 64]


def pack_weight(w):
    k, n = w.shape
    w = f64(np.asarray(w, np.float32).astype(ml_dtypes.bfloat16)).reshape(k // 32, 32, n)
    amax = np.abs(w).max(1)
    byte = np.clip(np.where(amax > 0, np.frexp(amax)[1] - 1 + 127 - 7, 1), 1, 254)
    scaled = (w * np.exp2(127.0 - byte)[:, None, :]).reshape(k, n).astype(np.float32)
    words = np.ascontiguousarray(scaled.reshape(k // 512, 128, 4, n).transpose(0, 1, 3, 2)).astype(ml_dtypes.float8_e4m3fn).view(np.uint8)
    return words, np.ascontiguousarray(byte.astype(np.uint8).reshape(k // 512, 16, n))


def unpack_weight(words, scales):
    g, p, n, _ = words.shape
    vals = np.ascontiguousarray(words).view(ml_dtypes.float8_e4m3fn).astype(np.float64) * np.repeat(np.exp2(scales.astype(np.float64) - 127.0), 8, axis=1)[..., None]
    return vals.transpose(0, 1, 3, 2).reshape(g * 512, n)


K, T, S, N, H = 512, 2048, 512, 512, 512


def setup_inputs():
    n = np.random.standard_normal
    s = mx_kscale(K)[:, None]
    u = mx_kscale(H)
    packed_xT = pack_weight(n((K, T)) * s)
    return {
        "x_words": packed_xT[0],
        "x_scales": packed_xT[1],
        "w1": (n((K, H)) / np.sqrt(K) / s).astype(np.float32),
        "w2": (n((K, H)) / np.sqrt(K) / s).astype(np.float32),
        "gn": (np.random.uniform(0.5, 1.5, (H, 1)) * u[:, None]).astype(np.float32),
        "w3": (n((H, N)) / np.sqrt(H) / u[:, None]).astype(np.float32),
        "offs": striped(np.random.permutation(T)[:S]),
        "p1": striped8(np.stack([np.random.permutation(S) for _ in range(8)])),
        "r1": striped8(np.stack([np.random.permutation(S) for _ in range(8)])),
        "p2": striped8(np.stack([np.random.permutation(S) for _ in range(8)])),
        "r2": striped8(np.stack([np.random.permutation(S) for _ in range(8)])),
    }


def reference(x_words, x_scales, w1, w2, gn, w3, offs, p1, r1, p2, r2):
    xq = unpack_weight(x_words, x_scales)[:, unstriped(offs)]
    y = mxq(f64(w1), 0, "e4m3").T @ xq
    e = mxq(f64(w2), 0, "e4m3").T @ xq
    z = f64(gn) * (y + np.clip(y[np.arange(H)[:, None], runs(p1, H)] - (e[np.arange(H)[:, None], runs(r1, H)]), -0.75, 0.75) + np.clip(y[np.arange(H)[:, None], runs(p2, H)] - (e[np.arange(H)[:, None], runs(r2, H)]), -0.75, 0.75))
    return mxq(f64(w3), 0, "e4m3").T @ mxq(z, 0, "e4m3")

@@ -1,0 +1,200 @@
+from contextlib import ExitStack
+
+import concourse.mybir as mybir
+
+K, T, S, N, H = 512, 2048, 512, 512, 512
+FLOPS = 2 * K * H * S * 2 + 2 * H * N * S
+
+F32 = mybir.dt.float32
+BF16 = mybir.dt.bfloat16
+I32 = mybir.dt.int32
+U32 = mybir.dt.uint32
+U16 = mybir.dt.uint16
+U8 = mybir.dt.uint8
+FP8X4 = mybir.dt.float8_e4m3fn_x4
+ALU = mybir.AluOpType
+ACT = mybir.ActivationFunctionType
+
+P = 128
+PACK = 4
+CLIP = 0.75
+CHUNK = 256
+LIST_COLS = S // 16
+
+
+def tile_picked_bpclip_none_p_kernel(
+    tc, x_words, x_scales, w1, w2, gn, w3, offs, p1, r1, p2, r2, out
+):
+    nc = tc.nc
+    with ExitStack() as ctx:
+        keep = ctx.enter_context(tc.tile_pool(name="keep", bufs=1))
+        ring = ctx.enter_context(tc.tile_pool(name="ring", bufs=4))
+        pair = ctx.enter_context(tc.tile_pool(name="pair", bufs=2))
+        psum = ctx.enter_context(tc.psum_pool(name="psum", bufs=4))
+        psum_out = ctx.enter_context(tc.psum_pool(name="psum_out", bufs=4))
+
+        def load_list(src, name):
+            tile = keep.tile([P, LIST_COLS], U16, name=name)
+            nc.sync.dma_start(tile[:], src)
+            return tile
+
+        def load_rows(w, name):
+            raw = keep.tile([P, PACK, w.shape[1]], F32, name=name)
+            nc.sync.dma_start(raw[:], w.rearrange("(p j) c -> p j c", j=PACK))
+            return raw
+
+        def quantize(grouped, width, pool, name):
+            codes = pool.tile([P, width], U32, name=name + "_codes", align_bytes=64)
+            scales = pool.tile([P, width], U8, name=name + "_scales", align_bytes=64)
+            nc.vector.quantize_mx(out=codes[:].bitcast(FP8X4), scales=scales[:], in_=grouped[:])
+            return codes, scales
+
+        def dealt_views(raw, name):
+            grouped = keep.tile([P, PACK * H], BF16, name=name, align_bytes=64)
+            dst = grouped[:].rearrange("p (t m j) -> p m j t", t=PACK, j=PACK)
+            src = raw[:].rearrange("p j (m t) -> p m j t", t=PACK)
+            return grouped, dst, src
+
+        def product(acc, lhs, cols, rhs):
+            nc.tensor.matmul_mx(
+                out=acc,
+                lhsT=lhs[0][:, cols].bitcast(FP8X4),
+                lhsT_scale=lhs[1][:, cols],
+                rhs=rhs[0][:].bitcast(FP8X4),
+                rhs_scale=rhs[1][:],
+                start=True,
+                stop=True,
+            )
+
+        scale_table = keep.tile([P, T], U8, name="scale_table")
+        nc.vector.memset(scale_table[:].bitcast(I32), 0)
+        gain = keep.tile([P, PACK], F32, name="gain")
+        nc.sync.dma_start(gain[:], gn.rearrange("(p t) o -> p (t o)", t=PACK))
+        offs_t = load_list(offs, "offs_t")
+        w1_raw = load_rows(w1, "w1_raw")
+        for q in range(4):
+            nc.sync.dma_start(
+                scale_table[32 * q : 32 * q + 4, :].bitcast(I32),
+                x_scales[0, 4 * q : 4 * q + 4, :].bitcast(I32),
+            )
+        word_table = keep.tile([P, T], U32, name="word_table")
+        nc.sync.dma_start(
+            word_table[:].bitcast(I32), x_words[0].rearrange("p c r -> p (c r)").bitcast(I32)
+        )
+        w2_raw = load_rows(w2, "w2_raw")
+        p_lists = [load_list(p1, "p1_t"), load_list(p2, "p2_t")]
+        r_lists = [load_list(r1, "r1_t"), load_list(r2, "r2_t")]
+        w3_raw = load_rows(w3, "w3_raw")
+
+        bound = keep.tile([P, PACK], F32, name="bound")
+        nc.scalar.activation(bound[:], gain[:], ACT.Abs, scale=CLIP)
+        span = keep.tile([P, PACK], F32, name="span")
+        nc.scalar.activation(span[:], gain[:], ACT.Abs, scale=2 * CLIP)
+
+        w1_grouped, dst, src = dealt_views(w1_raw, "w1_grouped")
+        nc.vector.tensor_copy(dst, src)
+        x_scale = keep.tile([P, S], U8, name="x_scale", align_bytes=64)
+        nc.vector.tensor_copy(x_scale[:], scale_table[:].indirect(offs_t[:]))
+        w1_q = quantize(w1_grouped, H, keep, "w1")
+        x_code = keep.tile([P, S], U32, name="x_code", align_bytes=64)
+        nc.vector.tensor_copy(x_code[:], word_table[:].indirect(offs_t[:]))
+        x_q = (x_code, x_scale)
+
+        def first_layer(w_q, t, name):
+            acc = psum.tile([P, S], F32, name="acc")
+            product(acc[:], w_q, slice(t * P, (t + 1) * P), x_q)
+            rows = keep.tile([P, S], F32, name=name)
+            nc.scalar.activation(rows[:], acc[:], ACT.Copy, scale=gain[:, t : t + 1])
+            return rows
+
+        chunks = range(S // CHUNK)
+
+        def list_slice(tile, c):
+            return tile[:, c * CHUNK // 16 : (c + 1) * CHUNK // 16]
+
+        beliefs, fetched = {}, {}
+
+        def fetch_beliefs(t):
+            for c in chunks:
+                for d in range(2):
+                    g = keep.tile([P, CHUNK], F32, name=f"fetched_{t}_{c}_{d}")
+                    nc.vector.tensor_copy(g[:], beliefs[t][:].indirect(list_slice(p_lists[d], c)))
+                    fetched[t, c, d] = g
+
+        for t in range(2):
+            beliefs[t] = first_layer(w1_q, t, f"belief_{t}")
+            fetch_beliefs(t)
+        w2_grouped, dst, src = dealt_views(w2_raw, "w2_grouped")
+        nc.scalar.copy(dst, src)
+        w2_q = quantize(w2_grouped, H, keep, "w2")
+        for t in range(2, PACK):
+            beliefs[t] = first_layer(w1_q, t, f"belief_{t}")
+            fetch_beliefs(t)
+        messages = [first_layer(w2_q, t, f"message_{t}") for t in range(PACK)]
+
+        w3_grouped = keep.tile([P, PACK * N], BF16, name="w3_grouped", align_bytes=64)
+        nc.scalar.copy(
+            w3_grouped[:].rearrange("p (c i j) -> p c j i", i=4, j=PACK),
+            w3_raw[:].rearrange("p j (c i) -> p c j i", i=4),
+        )
+        w3_q = quantize(w3_grouped, N, keep, "w3")
+
+        planes = {}
+
+        def differences(c, t):
+            lows = []
+            for d in range(2):
+                low = ring.tile([P, CHUNK], F32, name="low")
+                nc.vector.tensor_tensor(
+                    low[:], messages[t][:].indirect(list_slice(r_lists[d], c)), fetched[t, c, d][:], ALU.subtract
+                )
+                nc.scalar.activation(
+                    low[:], low[:], ACT.Relu, bias=bound[:, t : t + 1], scale=(1.0, -1.0)[d]
+                )
+                lows.append(low)
+            return lows
+
+        def combine(c, t, lows):
+            if t == 0:
+                planes[c] = pair.tile([P, PACK, CHUNK], BF16, name="planes")
+            part = pair.tile([P, CHUNK], F32, name="part")
+            nc.vector.scalar_tensor_tensor(
+                part[:], lows[0][:], span[:, t : t + 1], beliefs[t][:, c * CHUNK : (c + 1) * CHUNK], ALU.min, ALU.subtract
+            )
+            nc.vector.scalar_tensor_tensor(
+                planes[c][:, t, :], lows[1][:], span[:, t : t + 1], part[:], ALU.min, ALU.subtract
+            )
+
+        def last_layer(c):
+            z_grouped = pair.tile([P, PACK * CHUNK], BF16, name="z_grouped", align_bytes=64)
+            dst = z_grouped[:].rearrange("p (c i t) -> p c t i", i=4, t=PACK)
+            src = planes[c][:].rearrange("p t (c i) -> p c t i", i=4)
+            if c == chunks[-1]:
+                nc.vector.tensor_copy(dst, src)
+            else:
+                nc.scalar.copy(dst, src)
+            z_q = quantize(z_grouped, CHUNK, pair, "z")
+            for half in range(2):
+                acc = psum_out.tile([P, 2, CHUNK], F32, name="acc_out")
+                for u in range(2):
+                    m = 2 * half + u
+                    product(acc[:, u, :], w3_q, slice(m * P, (m + 1) * P), z_q)
+                result = ring.tile([P, 2, CHUNK], F32, name="result")
+                if c == chunks[-1] and half == 1:
+                    nc.vector.tensor_copy(result[:], acc[:])
+                else:
+                    nc.scalar.copy(result[:], acc[:])
+                rows = out[half * 2 * P : (half + 1) * 2 * P, c * CHUNK : (c + 1) * CHUNK]
+                nc.sync.dma_start(rows.rearrange("(u p) j -> p u j", p=P), result[:])
+
+        steps = [(c, t) for c in chunks for t in range(PACK)]
+        pending = None
+        for c, t in steps:
+            lows = differences(c, t)
+            if pending is not None:
+                combine(*pending)
+                if pending[1] == PACK - 1:
+                    last_layer(pending[0])
+            pending = (c, t, lows)
+        combine(*pending)
+        last_layer(pending[0])

@@ -1,6 +1,7 @@
 from contextlib import ExitStack
 
 import concourse.mybir as mybir
+from concourse.masks import make_identity
 
 K, T, S, N, H = 512, 2048, 512, 512, 512
 FLOPS = 2 * K * H * S * 2 + 2 * H * N * S
@@ -18,7 +19,8 @@ ACT = mybir.ActivationFunctionType
 P = 128
 PACK = 4
 CLIP = 0.75
-CHUNK = 256
+CHUNKS = ((0, 256), (256, 128), (384, 128))
+WIDE = 2 * S
 LIST_COLS = S // 16
 
 
@@ -30,17 +32,20 @@ def tile_picked_bpclip_none_p_kernel(
         keep = ctx.enter_context(tc.tile_pool(name="keep", bufs=1))
         ring = ctx.enter_context(tc.tile_pool(name="ring", bufs=4))
         pair = ctx.enter_context(tc.tile_pool(name="pair", bufs=2))
-        psum = ctx.enter_context(tc.psum_pool(name="psum", bufs=4))
-        psum_out = ctx.enter_context(tc.psum_pool(name="psum_out", bufs=4))
+        psum = ctx.enter_context(tc.psum_pool(name="psum", bufs=2))
+        psum_turn = ctx.enter_context(tc.psum_pool(name="psum_turn", bufs=3))
 
         def load_list(src, name):
             tile = keep.tile([P, LIST_COLS], U16, name=name)
             nc.sync.dma_start(tile[:], src)
             return tile
 
-        def load_rows(w, name):
+        def load_rows(w, name, pieces=1):
             raw = keep.tile([P, PACK, w.shape[1]], F32, name=name)
-            nc.sync.dma_start(raw[:], w.rearrange("(p j) c -> p j c", j=PACK))
+            rows = w.rearrange("(p j) c -> p j c", j=PACK)
+            step = PACK // pieces
+            for j in range(0, PACK, step):
+                nc.sync.dma_start(raw[:, j : j + step, :], rows[:, j : j + step, :])
             return raw
 
         def quantize(grouped, width, pool, name):
@@ -49,11 +54,13 @@ def tile_picked_bpclip_none_p_kernel(
             nc.vector.quantize_mx(out=codes[:].bitcast(FP8X4), scales=scales[:], in_=grouped[:])
             return codes, scales
 
-        def dealt_views(raw, name):
-            grouped = keep.tile([P, PACK * H], BF16, name=name, align_bytes=64)
-            dst = grouped[:].rearrange("p (t m j) -> p m j t", t=PACK, j=PACK)
-            src = raw[:].rearrange("p j (m t) -> p m j t", t=PACK)
-            return grouped, dst, src
+        def deal_columns(raw, u, tag, copy):
+            grouped = keep.tile([P, 2 * P * PACK], BF16, name="dealt", tag=tag, align_bytes=64)
+            copy(
+                grouped[:].rearrange("p (e m j) -> p m j e", e=2, j=PACK),
+                raw[:].rearrange("p j (m t) -> p m j t", t=PACK)[:, :, :, 2 * u : 2 * u + 2],
+            )
+            return grouped
 
         def product(acc, lhs, cols, rhs):
             nc.tensor.matmul_mx(
@@ -66,71 +73,86 @@ def tile_picked_bpclip_none_p_kernel(
                 stop=True,
             )
 
-        scale_table = keep.tile([P, T], U8, name="scale_table")
+        scale_table = keep.tile([P, T], U8, name="scale_table", tag="w1_0_codes", align_bytes=64)
         nc.vector.memset(scale_table[:].bitcast(I32), 0)
         gain = keep.tile([P, PACK], F32, name="gain")
         nc.sync.dma_start(gain[:], gn.rearrange("(p t) o -> p (t o)", t=PACK))
         offs_t = load_list(offs, "offs_t")
         w1_raw = load_rows(w1, "w1_raw")
+        p_lists = [load_list(p1, "p1_t"), load_list(p2, "p2_t")]
         for q in range(4):
             nc.sync.dma_start(
                 scale_table[32 * q : 32 * q + 4, :].bitcast(I32),
                 x_scales[0, 4 * q : 4 * q + 4, :].bitcast(I32),
             )
-        word_table = keep.tile([P, T], U32, name="word_table")
+        word_table = keep.tile([P, T], U32, name="word_table", tag="w1_dealt_1", align_bytes=64)
         nc.sync.dma_start(
             word_table[:].bitcast(I32), x_words[0].rearrange("p c r -> p (c r)").bitcast(I32)
         )
         w2_raw = load_rows(w2, "w2_raw")
-        p_lists = [load_list(p1, "p1_t"), load_list(p2, "p2_t")]
         r_lists = [load_list(r1, "r1_t"), load_list(r2, "r2_t")]
         w3_raw = load_rows(w3, "w3_raw")
 
-        bound = keep.tile([P, PACK], F32, name="bound")
-        nc.scalar.activation(bound[:], gain[:], ACT.Abs, scale=CLIP)
-        span = keep.tile([P, PACK], F32, name="span")
-        nc.scalar.activation(span[:], gain[:], ACT.Abs, scale=2 * CLIP)
+        identity = keep.tile([P, P], F32, name="identity")
+        make_identity(nc, identity[:])
 
-        w1_grouped, dst, src = dealt_views(w1_raw, "w1_grouped")
-        nc.vector.tensor_copy(dst, src)
+        def window(name, width):
+            rows = keep.tile([P, width], F32, name=name)
+            if width > S:
+                nc.gpsimd.memset(rows[:, S:], 0.0)
+            return rows
+
+        beliefs = [window(f"belief_{t}", WIDE) for t in range(PACK)]
+        messages = [window(f"message_{t}", WIDE if t == 0 else S) for t in range(PACK)]
+
+        def column_table(name, source, func, scale):
+            table = keep.tile([P, PACK], F32, name=name)
+            nc.scalar.activation(table[:], source[:], func, scale=scale)
+            return table
+
+        span = column_table("span", gain, ACT.Abs, 2 * CLIP)
+        lift = column_table("lift", gain, ACT.Abs, 3 * CLIP)
+        neg_span = column_table("neg_span", span, ACT.Copy, -1.0)
+        neg_gain = column_table("neg_gain", gain, ACT.Copy, -1.0)
+
         x_scale = keep.tile([P, S], U8, name="x_scale", align_bytes=64)
         nc.vector.tensor_copy(x_scale[:], scale_table[:].indirect(offs_t[:]))
-        w1_q = quantize(w1_grouped, H, keep, "w1")
+        w1_q = [quantize(deal_columns(w1_raw, 0, "w1_dealt_0", nc.scalar.copy), 2 * P, keep, "w1_0")]
         x_code = keep.tile([P, S], U32, name="x_code", align_bytes=64)
         nc.vector.tensor_copy(x_code[:], word_table[:].indirect(offs_t[:]))
         x_q = (x_code, x_scale)
+        w1_q.append(quantize(deal_columns(w1_raw, 1, "w1_dealt_1", nc.vector.tensor_copy), 2 * P, keep, "w1_1"))
 
-        def first_layer(w_q, t, name):
+        def first_layer(w_q, t, rows, scale, bias):
+            u, e = divmod(t, 2)
             acc = psum.tile([P, S], F32, name="acc")
-            product(acc[:], w_q, slice(t * P, (t + 1) * P), x_q)
-            rows = keep.tile([P, S], F32, name=name)
-            nc.scalar.activation(rows[:], acc[:], ACT.Copy, scale=gain[:, t : t + 1])
-            return rows
+            product(acc[:], w_q[u], slice(e * P, (e + 1) * P), x_q)
+            nc.scalar.activation(
+                rows[t][:, :S], acc[:], ACT.Identity, bias=bias[:, t : t + 1], scale=scale[:, t : t + 1]
+            )
 
-        chunks = range(S // CHUNK)
-
-        def list_slice(tile, c):
-            return tile[:, c * CHUNK // 16 : (c + 1) * CHUNK // 16]
-
-        beliefs, fetched = {}, {}
+        fetched = {}
 
         def fetch_beliefs(t):
-            for c in chunks:
-                for d in range(2):
-                    g = keep.tile([P, CHUNK], F32, name=f"fetched_{t}_{c}_{d}")
-                    nc.vector.tensor_copy(g[:], beliefs[t][:].indirect(list_slice(p_lists[d], c)))
-                    fetched[t, c, d] = g
+            for d in range(2):
+                fetched[t, d] = keep.tile(
+                    [P, S], F32, name=f"fetched_{t}_{d}", tag=f"fetched_{t}_{d}", align_bytes=64
+                )
+                nc.vector.tensor_copy(fetched[t, d][:], beliefs[t][:].indirect(p_lists[d][:]))
 
         for t in range(2):
-            beliefs[t] = first_layer(w1_q, t, f"belief_{t}")
-            fetch_beliefs(t)
-        w2_grouped, dst, src = dealt_views(w2_raw, "w2_grouped")
-        nc.scalar.copy(dst, src)
-        w2_q = quantize(w2_grouped, H, keep, "w2")
+            first_layer(w1_q, t, beliefs, gain, neg_span)
+        fetch_beliefs(0)
+        w2_q = [quantize(deal_columns(w2_raw, 0, "fetched_1_0", nc.scalar.copy), 2 * P, keep, "w2_0")]
+        fetch_beliefs(1)
+        for t in range(2):
+            first_layer(w2_q, t, messages, neg_gain, lift)
+        w2_q.append(quantize(deal_columns(w2_raw, 1, "w2_dealt_1", nc.scalar.copy), 2 * P, keep, "w2_1"))
         for t in range(2, PACK):
-            beliefs[t] = first_layer(w1_q, t, f"belief_{t}")
+            first_layer(w1_q, t, beliefs, gain, neg_span)
             fetch_beliefs(t)
-        messages = [first_layer(w2_q, t, f"message_{t}") for t in range(PACK)]
+        for t in range(2, PACK):
+            first_layer(w2_q, t, messages, neg_gain, lift)
 
         w3_grouped = keep.tile([P, PACK * N], BF16, name="w3_grouped", align_bytes=64)
         nc.scalar.copy(
@@ -139,62 +161,90 @@ def tile_picked_bpclip_none_p_kernel(
         )
         w3_q = quantize(w3_grouped, N, keep, "w3")
 
-        planes = {}
+        last = len(CHUNKS) - 1
 
-        def differences(c, t):
-            lows = []
+        def differences(t, lo, width):
+            terms = ring.tile([P, 2, width], F32, name="terms")
             for d in range(2):
-                low = ring.tile([P, CHUNK], F32, name="low")
+                picks = r_lists[d][:, lo // 16 : (lo + width) // 16]
                 nc.vector.tensor_tensor(
-                    low[:], messages[t][:].indirect(list_slice(r_lists[d], c)), fetched[t, c, d][:], ALU.subtract
+                    terms[:, d, :], messages[t][:].indirect(picks), fetched[t, d][:, lo : lo + width], ALU.add
                 )
-                nc.scalar.activation(
-                    low[:], low[:], ACT.Relu, bias=bound[:, t : t + 1], scale=(1.0, -1.0)[d]
-                )
-                lows.append(low)
-            return lows
+            return terms
 
-        def combine(c, t, lows):
-            if t == 0:
-                planes[c] = pair.tile([P, PACK, CHUNK], BF16, name="planes")
-            part = pair.tile([P, CHUNK], F32, name="part")
-            nc.vector.scalar_tensor_tensor(
-                part[:], lows[0][:], span[:, t : t + 1], beliefs[t][:, c * CHUNK : (c + 1) * CHUNK], ALU.min, ALU.subtract
-            )
-            nc.vector.scalar_tensor_tensor(
-                planes[c][:, t, :], lows[1][:], span[:, t : t + 1], part[:], ALU.min, ALU.subtract
-            )
+        def clip(t, terms, on_vector):
+            col = slice(t, t + 1)
+            flat = terms[:].rearrange("p d n -> p (d n)")
+            if on_vector:
+                nc.vector.tensor_scalar(flat, flat, 0.0, span[:, col], ALU.max, ALU.min)
+            else:
+                for step in range(2):
+                    nc.scalar.activation(flat, flat, ACT.Relu, bias=span[:, col], scale=-1.0)
+
+        sums, words = {}, {}
+
+        def add_turned(t, c, terms, terms_lo):
+            u, e = divmod(t, 2)
+            lo, width = CHUNKS[c]
+            if e == 0:
+                sums[c, u] = psum_turn.tile([P, width // P, 2, P], F32, name="turned_sum")
+            for b in range(width // P):
+                tok = lo + b * P
+                parts = [beliefs[t][:, tok : tok + P]]
+                parts += [terms[:, d, tok - terms_lo : tok - terms_lo + P] for d in range(2)]
+                for i, part in enumerate(parts):
+                    nc.tensor.matmul(
+                        sums[c, u][:, b, e, :], part, identity[:], start=(i == 0), stop=(i == 2), is_transpose=True
+                    )
+
+        def turn_back(c, u):
+            blocks = CHUNKS[c][1] // P
+            z_rows = pair.tile([P, blocks, P, 2], BF16, name="z_rows")
+            nc.scalar.copy(z_rows[:], sums[c, u][:].rearrange("n b e p -> n b p e"))
+            if u == 0:
+                words[c] = psum_turn.tile([P, blocks, 2, P], F32, name="words")
+            z_words = z_rows[:].rearrange("n b p e -> n (b p e)").bitcast(F32)
+            for b in range(blocks):
+                nc.tensor.transpose(words[c][:, b, u, :], z_words[:, b * P : (b + 1) * P], identity[:])
 
         def last_layer(c):
-            z_grouped = pair.tile([P, PACK * CHUNK], BF16, name="z_grouped", align_bytes=64)
-            dst = z_grouped[:].rearrange("p (c i t) -> p c t i", i=4, t=PACK)
-            src = planes[c][:].rearrange("p t (c i) -> p c t i", i=4)
-            if c == chunks[-1]:
+            lo, width = CHUNKS[c]
+            z_grouped = pair.tile([P, PACK * width], BF16, name="z_grouped", align_bytes=64)
+            dst = z_grouped[:].bitcast(F32).rearrange("p (b n u) -> p b n u", n=P, u=2)
+            src = words[c][:].rearrange("p b u n -> p b n u")
+            if c == last:
                 nc.vector.tensor_copy(dst, src)
             else:
                 nc.scalar.copy(dst, src)
-            z_q = quantize(z_grouped, CHUNK, pair, "z")
+            z_q = quantize(z_grouped, width, pair, "z")
             for half in range(2):
-                acc = psum_out.tile([P, 2, CHUNK], F32, name="acc_out")
-                for u in range(2):
-                    m = 2 * half + u
-                    product(acc[:, u, :], w3_q, slice(m * P, (m + 1) * P), z_q)
-                result = ring.tile([P, 2, CHUNK], F32, name="result")
-                if c == chunks[-1] and half == 1:
+                acc = psum.tile([P, 2, width], F32, name="acc")
+                for i in range(2):
+                    m = 2 * half + i
+                    product(acc[:, i, :], w3_q, slice(m * P, (m + 1) * P), z_q)
+                result = ring.tile([P, 2, width], F32, name="result")
+                if c == last and half == 1:
                     nc.vector.tensor_copy(result[:], acc[:])
                 else:
                     nc.scalar.copy(result[:], acc[:])
-                rows = out[half * 2 * P : (half + 1) * 2 * P, c * CHUNK : (c + 1) * CHUNK]
-                nc.sync.dma_start(rows.rearrange("(u p) j -> p u j", p=P), result[:])
+                rows = out[half * 2 * P : (half + 1) * 2 * P, lo : lo + width]
+                nc.sync.dma_start(rows.rearrange("(i p) j -> p i j", p=P), result[:])
 
-        steps = [(c, t) for c in chunks for t in range(PACK)]
+        def finish(t, group, terms):
+            clip(t, terms, t == PACK - 1 or (t == 2 and group[0] > 0))
+            for c in group:
+                add_turned(t, c, terms, CHUNKS[group[0]][0])
+                if t % 2 == 1:
+                    turn_back(c, t // 2)
+                if t == PACK - 1:
+                    last_layer(c)
+
+        steps = [(0, (0, 1, 2)), (1, (0,)), (2, (0,)), (3, (0,)), (1, (1, 2))]
+        steps += [(t, (c,)) for c in (1, 2) for t in (2, 3)]
         pending = None
-        for c, t in steps:
-            lows = differences(c, t)
+        for t, group in steps:
+            terms = differences(t, CHUNKS[group[0]][0], sum(CHUNKS[c][1] for c in group))
             if pending is not None:
-                combine(*pending)
-                if pending[1] == PACK - 1:
-                    last_layer(pending[0])
-            pending = (c, t, lows)
-        combine(*pending)
-        last_layer(pending[0])
+                finish(*pending)
+            pending = (t, group, terms)
+        finish(*pending)

@@ -19,7 +19,7 @@ ACT = mybir.ActivationFunctionType
 P = 128
 PACK = 4
 CLIP = 0.75
-CHUNKS = ((0, 256), (256, 128), (384, 128))
+HALF = S // 2
 WIDE = 2 * S
 LIST_COLS = S // 16
 
@@ -32,8 +32,8 @@ def tile_picked_bpclip_none_p_kernel(
         keep = ctx.enter_context(tc.tile_pool(name="keep", bufs=1))
         ring = ctx.enter_context(tc.tile_pool(name="ring", bufs=4))
         pair = ctx.enter_context(tc.tile_pool(name="pair", bufs=2))
-        psum = ctx.enter_context(tc.psum_pool(name="psum", bufs=2))
-        psum_turn = ctx.enter_context(tc.psum_pool(name="psum_turn", bufs=3))
+        psum = ctx.enter_context(tc.psum_pool(name="psum", bufs=4))
+        psum_turn = ctx.enter_context(tc.psum_pool(name="psum_turn", bufs=2))
 
         def load_list(src, name):
             tile = keep.tile([P, LIST_COLS], U16, name=name)
@@ -51,7 +51,7 @@ def tile_picked_bpclip_none_p_kernel(
         def quantize(grouped, width, pool, name):
             codes = pool.tile([P, width], U32, name=name + "_codes", align_bytes=64)
             scales = pool.tile([P, width], U8, name=name + "_scales", align_bytes=64)
-            nc.vector.quantize_mx(out=codes[:].bitcast(FP8X4), scales=scales[:], in_=grouped[:])
+            nc.vector.quantize_mx(out=codes[:].bitcast(FP8X4), scales=scales[:], in_=grouped)
             return codes, scales
 
         def deal_columns(raw, u, tag, copy):
@@ -60,15 +60,15 @@ def tile_picked_bpclip_none_p_kernel(
                 grouped[:].rearrange("p (e m j) -> p m j e", e=2, j=PACK),
                 raw[:].rearrange("p j (m t) -> p m j t", t=PACK)[:, :, :, 2 * u : 2 * u + 2],
             )
-            return grouped
+            return grouped[:]
 
-        def product(acc, lhs, cols, rhs):
+        def product(acc, lhs, cols, rhs, rhs_cols=slice(None)):
             nc.tensor.matmul_mx(
                 out=acc,
                 lhsT=lhs[0][:, cols].bitcast(FP8X4),
                 lhsT_scale=lhs[1][:, cols],
-                rhs=rhs[0][:].bitcast(FP8X4),
-                rhs_scale=rhs[1][:],
+                rhs=rhs[0][:, rhs_cols].bitcast(FP8X4),
+                rhs_scale=rhs[1][:, rhs_cols],
                 start=True,
                 stop=True,
             )
@@ -79,7 +79,6 @@ def tile_picked_bpclip_none_p_kernel(
         nc.sync.dma_start(gain[:], gn.rearrange("(p t) o -> p (t o)", t=PACK))
         offs_t = load_list(offs, "offs_t")
         w1_raw = load_rows(w1, "w1_raw")
-        p_lists = [load_list(p1, "p1_t"), load_list(p2, "p2_t")]
         for q in range(4):
             nc.sync.dma_start(
                 scale_table[32 * q : 32 * q + 4, :].bitcast(I32),
@@ -90,6 +89,7 @@ def tile_picked_bpclip_none_p_kernel(
             word_table[:].bitcast(I32), x_words[0].rearrange("p c r -> p (c r)").bitcast(I32)
         )
         w2_raw = load_rows(w2, "w2_raw")
+        p_lists = [load_list(p1, "p1_t"), load_list(p2, "p2_t")]
         r_lists = [load_list(r1, "r1_t"), load_list(r2, "r2_t")]
         w3_raw = load_rows(w3, "w3_raw")
 
@@ -97,7 +97,7 @@ def tile_picked_bpclip_none_p_kernel(
         make_identity(nc, identity[:])
 
         def window(name, width):
-            rows = keep.tile([P, width], F32, name=name)
+            rows = keep.tile([P, width], F32, name=name, align_bytes=64)
             if width > S:
                 nc.gpsimd.memset(rows[:, S:], 0.0)
             return rows
@@ -119,38 +119,41 @@ def tile_picked_bpclip_none_p_kernel(
         nc.vector.tensor_copy(x_scale[:], scale_table[:].indirect(offs_t[:]))
         w1_q = [quantize(deal_columns(w1_raw, 0, "w1_dealt_0", nc.scalar.copy), 2 * P, keep, "w1_0")]
         x_code = keep.tile([P, S], U32, name="x_code", align_bytes=64)
-        nc.vector.tensor_copy(x_code[:], word_table[:].indirect(offs_t[:]))
+        for half in range(2):
+            nc.vector.tensor_copy(
+                x_code[:, half * S // 2 : (half + 1) * S // 2],
+                word_table[:].indirect(offs_t[:, half * LIST_COLS // 2 : (half + 1) * LIST_COLS // 2]),
+            )
         x_q = (x_code, x_scale)
         w1_q.append(quantize(deal_columns(w1_raw, 1, "w1_dealt_1", nc.vector.tensor_copy), 2 * P, keep, "w1_1"))
 
-        def first_layer(w_q, t, rows, scale, bias):
+        def first_layer(w_q, t, rows, scale, bias, pieces=1):
             u, e = divmod(t, 2)
-            acc = psum.tile([P, S], F32, name="acc")
-            product(acc[:], w_q[u], slice(e * P, (e + 1) * P), x_q)
-            nc.scalar.activation(
-                rows[t][:, :S], acc[:], ACT.Identity, bias=bias[:, t : t + 1], scale=scale[:, t : t + 1]
-            )
+            width = S // pieces
+            for lo in range(0, S, width):
+                acc = psum.tile([P, width], F32, name="acc")
+                product(acc[:], w_q[u], slice(e * P, (e + 1) * P), x_q, slice(lo, lo + width))
+                nc.scalar.activation(
+                    rows[t][:, lo : lo + width], acc[:], ACT.Identity, bias=bias[:, t : t + 1], scale=scale[:, t : t + 1]
+                )
 
         fetched = {}
 
-        def fetch_beliefs(t):
+        def fetch_beliefs(t, tag):
+            fetched[t] = keep.tile([P, 2, S], F32, name=f"fetched_{t}", tag=tag, align_bytes=64)
             for d in range(2):
-                fetched[t, d] = keep.tile(
-                    [P, S], F32, name=f"fetched_{t}_{d}", tag=f"fetched_{t}_{d}", align_bytes=64
-                )
-                nc.vector.tensor_copy(fetched[t, d][:], beliefs[t][:].indirect(p_lists[d][:]))
+                nc.vector.tensor_copy(fetched[t][:, d, :], beliefs[t][:].indirect(p_lists[d][:]))
 
-        for t in range(2):
-            first_layer(w1_q, t, beliefs, gain, neg_span)
-        fetch_beliefs(0)
-        w2_q = [quantize(deal_columns(w2_raw, 0, "fetched_1_0", nc.scalar.copy), 2 * P, keep, "w2_0")]
-        fetch_beliefs(1)
+        first_layer(w1_q, 0, beliefs, gain, neg_span, pieces=2)
+        first_layer(w1_q, 1, beliefs, gain, neg_span)
+        fetch_beliefs(0, "fetched_0")
+        w2_q = [quantize(deal_columns(w2_raw, 0, "fetched_1", nc.scalar.copy), 2 * P, keep, "w2_0")]
+        fetch_beliefs(1, "fetched_1")
         for t in range(2):
             first_layer(w2_q, t, messages, neg_gain, lift)
         w2_q.append(quantize(deal_columns(w2_raw, 1, "w2_dealt_1", nc.scalar.copy), 2 * P, keep, "w2_1"))
         for t in range(2, PACK):
             first_layer(w1_q, t, beliefs, gain, neg_span)
-            fetch_beliefs(t)
         for t in range(2, PACK):
             first_layer(w2_q, t, messages, neg_gain, lift)
 
@@ -159,92 +162,117 @@ def tile_picked_bpclip_none_p_kernel(
             w3_grouped[:].rearrange("p (c i j) -> p c j i", i=4, j=PACK),
             w3_raw[:].rearrange("p j (c i) -> p c j i", i=4),
         )
-        w3_q = quantize(w3_grouped, N, keep, "w3")
-
-        last = len(CHUNKS) - 1
+        w3_q = quantize(w3_grouped[:], N, keep, "w3")
 
         def differences(t, lo, width):
-            terms = ring.tile([P, 2, width], F32, name="terms")
+            if lo + width == S and t == PACK - 1:
+                terms = keep.tile([P, 2, width], F32, name="last_terms", tag="z_grouped_0", align_bytes=64)
+            else:
+                terms = ring.tile([P, 2, width], F32, name="terms")
             for d in range(2):
                 picks = r_lists[d][:, lo // 16 : (lo + width) // 16]
                 nc.vector.tensor_tensor(
-                    terms[:, d, :], messages[t][:].indirect(picks), fetched[t, d][:, lo : lo + width], ALU.add
+                    terms[:, d, :], messages[t][:].indirect(picks), fetched[t][:, d, lo : lo + width], ALU.add
                 )
             return terms
 
-        def clip(t, terms, on_vector):
+        def clip(t, terms):
             col = slice(t, t + 1)
             flat = terms[:].rearrange("p d n -> p (d n)")
-            if on_vector:
+            if t == PACK - 1:
                 nc.vector.tensor_scalar(flat, flat, 0.0, span[:, col], ALU.max, ALU.min)
             else:
                 for step in range(2):
                     nc.scalar.activation(flat, flat, ACT.Relu, bias=span[:, col], scale=-1.0)
 
+        blocks = HALF // P
         sums, words = {}, {}
+        grouped = [keep.tile([P, HALF, PACK], BF16, name=f"z_grouped_{h}", align_bytes=64) for h in range(2)]
+        planes = keep.tile([P, 2, HALF], BF16, name="planes")
 
-        def add_turned(t, c, terms, terms_lo):
+        def add_turned(t, h, terms, terms_lo):
             u, e = divmod(t, 2)
-            lo, width = CHUNKS[c]
             if e == 0:
-                sums[c, u] = psum_turn.tile([P, width // P, 2, P], F32, name="turned_sum")
-            for b in range(width // P):
-                tok = lo + b * P
+                sums[h, u] = psum_turn.tile([P, blocks, 2, P], F32, name="turned_sum")
+            for b in range(blocks):
+                tok = h * HALF + b * P
                 parts = [beliefs[t][:, tok : tok + P]]
                 parts += [terms[:, d, tok - terms_lo : tok - terms_lo + P] for d in range(2)]
                 for i, part in enumerate(parts):
                     nc.tensor.matmul(
-                        sums[c, u][:, b, e, :], part, identity[:], start=(i == 0), stop=(i == 2), is_transpose=True
+                        sums[h, u][:, b, e, :], part, identity[:], start=(i == 0), stop=(i == 2), is_transpose=True
                     )
 
-        def turn_back(c, u):
-            blocks = CHUNKS[c][1] // P
+        def turn_back(h, u):
             z_rows = pair.tile([P, blocks, P, 2], BF16, name="z_rows")
-            nc.scalar.copy(z_rows[:], sums[c, u][:].rearrange("n b e p -> n b p e"))
+            nc.scalar.copy(z_rows[:], sums[h, u][:].rearrange("n b e p -> n b p e"))
             if u == 0:
-                words[c] = psum_turn.tile([P, blocks, 2, P], F32, name="words")
+                words[h] = psum_turn.tile([P, blocks, 2, P], F32, name="words")
             z_words = z_rows[:].rearrange("n b p e -> n (b p e)").bitcast(F32)
             for b in range(blocks):
-                nc.tensor.transpose(words[c][:, b, u, :], z_words[:, b * P : (b + 1) * P], identity[:])
+                nc.tensor.transpose(words[h][:, b, u, :], z_words[:, b * P : (b + 1) * P], identity[:])
 
-        def last_layer(c):
-            lo, width = CHUNKS[c]
-            z_grouped = pair.tile([P, PACK * width], BF16, name="z_grouped", align_bytes=64)
-            dst = z_grouped[:].bitcast(F32).rearrange("p (b n u) -> p b n u", n=P, u=2)
-            src = words[c][:].rearrange("p b u n -> p b n u")
-            if c == last:
-                nc.vector.tensor_copy(dst, src)
+        def group_words(h, pairs):
+            dst = grouped[h][:].bitcast(F32).rearrange("p (b n) u -> p b n u", n=P)
+            nc.scalar.copy(dst[:, :, :, :pairs], words[h][:].rearrange("p b u n -> p b n u")[:, :, :, :pairs])
+
+        def add_on_vector(t, lo, width, terms):
+            col = slice(t, t + 1)
+            part = pair.tile([P, width], F32, name="part")
+            plane = planes[:, t - 2, lo - HALF : lo - HALF + width]
+            for d, (total, addend) in enumerate(((part[:], beliefs[t][:, lo : lo + width]), (plane, part[:]))):
+                nc.scalar.activation(terms[:, d, :], terms[:, d, :], ACT.Relu)
+                nc.vector.scalar_tensor_tensor(total, terms[:, d, :], span[:, col], addend, ALU.min, ALU.add)
+
+        def group_planes(lo, width, copy):
+            cols = slice(lo - HALF, lo - HALF + width)
+            copy(grouped[1][:, cols, 2:], planes[:, :, cols].rearrange("p e n -> p n e"))
+
+        def last_layer(lo, width, copies):
+            h, first = divmod(lo, HALF)
+            z_q = quantize(grouped[h][:, first : first + width, :].rearrange("p n t -> p (n t)"), width, pair, "z")
+            tiles = PACK // len(copies)
+            for i, copy in enumerate(copies):
+                acc = psum.tile([P, tiles, width], F32, name="acc")
+                for j in range(tiles):
+                    m = tiles * i + j
+                    product(acc[:, j, :], w3_q, slice(m * P, (m + 1) * P), z_q)
+                result = keep.tile([P, tiles, width], F32, name=f"result_{lo}_{i}")
+                copy(result[:], acc[:])
+                rows = out[i * tiles * P : (i + 1) * tiles * P, lo : lo + width]
+                nc.sync.dma_start(rows.rearrange("(j p) n -> p j n", p=P), result[:])
+
+        def finish(t, lo, width, terms):
+            if t >= 2 and lo >= HALF:
+                add_on_vector(t, lo, width, terms)
             else:
-                nc.scalar.copy(dst, src)
-            z_q = quantize(z_grouped, width, pair, "z")
-            for half in range(2):
-                acc = psum.tile([P, 2, width], F32, name="acc")
-                for i in range(2):
-                    m = 2 * half + i
-                    product(acc[:, i, :], w3_q, slice(m * P, (m + 1) * P), z_q)
-                result = ring.tile([P, 2, width], F32, name="result")
-                if c == last and half == 1:
-                    nc.vector.tensor_copy(result[:], acc[:])
-                else:
-                    nc.scalar.copy(result[:], acc[:])
-                rows = out[half * 2 * P : (half + 1) * 2 * P, lo : lo + width]
-                nc.sync.dma_start(rows.rearrange("(i p) j -> p i j", p=P), result[:])
+                clip(t, terms)
+                for h in range(lo // HALF, (lo + width) // HALF):
+                    add_turned(t, h, terms, lo)
+                    if t % 2 == 1:
+                        turn_back(h, t // 2)
+            if (t, lo) == (1, HALF):
+                group_words(1, 1)
+            if (t, lo) == (3, 0):
+                group_words(0, 2)
+                last_layer(lo, width, (nc.scalar.copy, nc.scalar.copy))
+            if (t, lo) == (3, HALF):
+                group_planes(lo, width, nc.scalar.copy)
+                last_layer(lo, width, (nc.scalar.copy,))
+            if (t, lo) == (3, HALF + P):
+                group_planes(lo, width, nc.vector.tensor_copy)
+                last_layer(lo, width, (nc.scalar.copy, nc.vector.tensor_copy))
 
-        def finish(t, group, terms):
-            clip(t, terms, t == PACK - 1 or (t == 2 and group[0] > 0))
-            for c in group:
-                add_turned(t, c, terms, CHUNKS[group[0]][0])
-                if t % 2 == 1:
-                    turn_back(c, t // 2)
-                if t == PACK - 1:
-                    last_layer(c)
-
-        steps = [(0, (0, 1, 2)), (1, (0,)), (2, (0,)), (3, (0,)), (1, (1, 2))]
-        steps += [(t, (c,)) for c in (1, 2) for t in (2, 3)]
+        steps = [(0, 0, S)] + [(t, 0, HALF) for t in (1, 2, 3)] + [(t, HALF, HALF) for t in (1, 2)]
+        steps += [(3, HALF, P), (3, HALF + P, P)]
         pending = None
-        for t, group in steps:
-            terms = differences(t, CHUNKS[group[0]][0], sum(CHUNKS[c][1] for c in group))
+        for step in steps:
+            terms = differences(*step)
+            if step == (1, 0, HALF):
+                fetch_beliefs(2, "fetched_0")
+            if step == (2, 0, HALF):
+                fetch_beliefs(3, "message_0")
             if pending is not None:
                 finish(*pending)
-            pending = (t, group, terms)
+            pending = (*step, terms)
         finish(*pending)

@@ -99,7 +99,7 @@ def tile_picked_bpclip_none_p_kernel(
         def window(name, width):
             rows = keep.tile([P, width], F32, name=name, align_bytes=64)
             if width > S:
-                nc.gpsimd.memset(rows[:, S:], 0.0)
+                nc.vector.memset(rows[:, S:], 0.0)
             return rows
 
         beliefs = [window(f"belief_{t}", WIDE) for t in range(PACK)]
@@ -176,10 +176,10 @@ def tile_picked_bpclip_none_p_kernel(
                 )
             return terms
 
-        def clip(t, terms):
+        def clip(t, terms, on_vector):
             col = slice(t, t + 1)
             flat = terms[:].rearrange("p d n -> p (d n)")
-            if t == PACK - 1:
+            if on_vector:
                 nc.vector.tensor_scalar(flat, flat, 0.0, span[:, col], ALU.max, ALU.min)
             else:
                 for step in range(2):
@@ -217,12 +217,9 @@ def tile_picked_bpclip_none_p_kernel(
             nc.scalar.copy(dst[:, :, :, :pairs], words[h][:].rearrange("p b u n -> p b n u")[:, :, :, :pairs])
 
         def add_on_vector(t, lo, width, terms):
-            col = slice(t, t + 1)
             part = pair.tile([P, width], F32, name="part")
-            plane = planes[:, t - 2, lo - HALF : lo - HALF + width]
-            for d, (total, addend) in enumerate(((part[:], beliefs[t][:, lo : lo + width]), (plane, part[:]))):
-                nc.scalar.activation(terms[:, d, :], terms[:, d, :], ACT.Relu)
-                nc.vector.scalar_tensor_tensor(total, terms[:, d, :], span[:, col], addend, ALU.min, ALU.add)
+            nc.vector.tensor_tensor(part[:], terms[:, 0, :], beliefs[t][:, lo : lo + width], ALU.add)
+            nc.vector.tensor_tensor(planes[:, t - 2, lo - HALF : lo - HALF + width], terms[:, 1, :], part[:], ALU.add)
 
         def group_planes(lo, width, copy):
             cols = slice(lo - HALF, lo - HALF + width)
@@ -243,10 +240,11 @@ def tile_picked_bpclip_none_p_kernel(
                 nc.sync.dma_start(rows.rearrange("(j p) n -> p j n", p=P), result[:])
 
         def finish(t, lo, width, terms):
-            if t >= 2 and lo >= HALF:
+            late = t >= 2 and lo >= HALF
+            clip(t, terms, late or t == PACK - 1)
+            if late:
                 add_on_vector(t, lo, width, terms)
             else:
-                clip(t, terms)
                 for h in range(lo // HALF, (lo + width) // HALF):
                     add_turned(t, h, terms, lo)
                     if t % 2 == 1:
@@ -275,4 +273,7 @@ def tile_picked_bpclip_none_p_kernel(
             if pending is not None:
                 finish(*pending)
             pending = (*step, terms)
+            if step == (3, 0, HALF):
+                finish(*pending)
+                pending = None
         finish(*pending)

@@ -164,26 +164,22 @@ def tile_picked_bpclip_none_p_kernel(
         )
         w3_q = quantize(w3_grouped[:], N, keep, "w3")
 
+        def difference(dst, t, d, lo, width):
+            picks = r_lists[d][:, lo // 16 : (lo + width) // 16]
+            nc.vector.tensor_tensor(dst, messages[t][:].indirect(picks), fetched[t][:, d, lo : lo + width], ALU.add)
+
         def differences(t, lo, width):
-            if lo + width == S and t == PACK - 1:
-                terms = keep.tile([P, 2, width], F32, name="last_terms", tag="z_grouped_0", align_bytes=64)
-            else:
-                terms = ring.tile([P, 2, width], F32, name="terms")
+            terms = ring.tile([P, 2, width], F32, name="terms")
             for d in range(2):
-                picks = r_lists[d][:, lo // 16 : (lo + width) // 16]
-                nc.vector.tensor_tensor(
-                    terms[:, d, :], messages[t][:].indirect(picks), fetched[t][:, d, lo : lo + width], ALU.add
-                )
+                difference(terms[:, d, :], t, d, lo, width)
             return terms
 
-        def clip(t, terms, on_vector):
-            col = slice(t, t + 1)
-            flat = terms[:].rearrange("p d n -> p (d n)")
-            if on_vector:
-                nc.vector.tensor_scalar(flat, flat, 0.0, span[:, col], ALU.max, ALU.min)
-            else:
-                for step in range(2):
-                    nc.scalar.activation(flat, flat, ACT.Relu, bias=span[:, col], scale=-1.0)
+        def clip_on_vector(t, flat):
+            nc.vector.tensor_scalar(flat, flat, 0.0, span[:, t : t + 1], ALU.max, ALU.min)
+
+        def clip_on_scalar(t, flat):
+            for step in range(2):
+                nc.scalar.activation(flat, flat, ACT.Relu, bias=span[:, t : t + 1], scale=-1.0)
 
         blocks = HALF // P
         sums, words = {}, {}
@@ -216,15 +212,6 @@ def tile_picked_bpclip_none_p_kernel(
             dst = grouped[h][:].bitcast(F32).rearrange("p (b n) u -> p b n u", n=P)
             nc.scalar.copy(dst[:, :, :, :pairs], words[h][:].rearrange("p b u n -> p b n u")[:, :, :, :pairs])
 
-        def add_on_vector(t, lo, width, terms):
-            part = pair.tile([P, width], F32, name="part")
-            nc.vector.tensor_tensor(part[:], terms[:, 0, :], beliefs[t][:, lo : lo + width], ALU.add)
-            nc.vector.tensor_tensor(planes[:, t - 2, lo - HALF : lo - HALF + width], terms[:, 1, :], part[:], ALU.add)
-
-        def group_planes(lo, width, copy):
-            cols = slice(lo - HALF, lo - HALF + width)
-            copy(grouped[1][:, cols, 2:], planes[:, :, cols].rearrange("p e n -> p n e"))
-
         def last_layer(lo, width, copies):
             h, first = divmod(lo, HALF)
             z_q = quantize(grouped[h][:, first : first + width, :].rearrange("p n t -> p (n t)"), width, pair, "z")
@@ -240,40 +227,51 @@ def tile_picked_bpclip_none_p_kernel(
                 nc.sync.dma_start(rows.rearrange("(j p) n -> p j n", p=P), result[:])
 
         def finish(t, lo, width, terms):
-            late = t >= 2 and lo >= HALF
-            clip(t, terms, late or t == PACK - 1)
-            if late:
-                add_on_vector(t, lo, width, terms)
-            else:
-                for h in range(lo // HALF, (lo + width) // HALF):
-                    add_turned(t, h, terms, lo)
-                    if t % 2 == 1:
-                        turn_back(h, t // 2)
-            if (t, lo) == (1, HALF):
-                group_words(1, 1)
-            if (t, lo) == (3, 0):
-                group_words(0, 2)
-                last_layer(lo, width, (nc.scalar.copy, nc.scalar.copy))
-            if (t, lo) == (3, HALF):
-                group_planes(lo, width, nc.scalar.copy)
-                last_layer(lo, width, (nc.scalar.copy,))
-            if (t, lo) == (3, HALF + P):
-                group_planes(lo, width, nc.vector.tensor_copy)
-                last_layer(lo, width, (nc.scalar.copy, nc.vector.tensor_copy))
+            clip = clip_on_vector if t == PACK - 1 else clip_on_scalar
+            clip(t, terms[:].rearrange("p d n -> p (d n)"))
+            for h in range(lo // HALF, (lo + width) // HALF):
+                add_turned(t, h, terms, lo)
+                if t % 2 == 1:
+                    turn_back(h, t // 2)
 
-        steps = [(0, 0, S)] + [(t, 0, HALF) for t in (1, 2, 3)] + [(t, HALF, HALF) for t in (1, 2)]
-        steps += [(3, HALF, P), (3, HALF + P, P)]
-        pending = None
-        for step in steps:
-            terms = differences(*step)
-            if step == (1, 0, HALF):
-                fetch_beliefs(2, "fetched_0")
-            if step == (2, 0, HALF):
-                fetch_beliefs(3, "message_0")
-            if pending is not None:
-                finish(*pending)
-            pending = (*step, terms)
-            if step == (3, 0, HALF):
-                finish(*pending)
-                pending = None
-        finish(*pending)
+        terms_0 = differences(0, 0, S)
+        terms_1 = differences(1, 0, HALF)
+        fetch_beliefs(2, "fetched_0")
+        finish(0, 0, S, terms_0)
+        terms_2 = differences(2, 0, HALF)
+        fetch_beliefs(3, "message_0")
+        finish(1, 0, HALF, terms_1)
+        terms_3 = differences(3, 0, HALF)
+        finish(2, 0, HALF, terms_2)
+        finish(3, 0, HALF, terms_3)
+        group_words(0, 2)
+        last_layer(0, HALF, (nc.scalar.copy, nc.scalar.copy))
+
+        terms_1 = differences(1, HALF, HALF)
+        terms_2 = differences(2, HALF, HALF)
+        finish(1, HALF, HALF, terms_1)
+        group_words(1, 1)
+
+        early_3 = ring.tile([P, HALF + P], F32, name="terms")
+        last_3 = keep.tile([P, P], F32, name="last_3", tag="z_grouped_0", align_bytes=64)
+        first_3, second_3 = early_3[:, :HALF], (early_3[:, HALF:], last_3[:])
+        part_2 = keep.tile([P, HALF], F32, name="part_2")
+        part_3 = keep.tile([P, HALF], F32, name="part_3")
+        difference(first_3, 3, 0, HALF, HALF)
+        clip_on_vector(2, terms_2[:].rearrange("p d n -> p (d n)"))
+        difference(second_3[0], 3, 1, HALF, P)
+        nc.vector.tensor_tensor(part_2[:], terms_2[:, 0, :], beliefs[2][:, HALF:S], ALU.add)
+        clip_on_vector(3, first_3)
+        nc.vector.tensor_tensor(planes[:, 0, :], terms_2[:, 1, :], part_2[:], ALU.add)
+        difference(second_3[1], 3, 1, HALF + P, P)
+        nc.vector.tensor_tensor(part_3[:], first_3, beliefs[3][:, HALF:S], ALU.add)
+        for b in range(blocks):
+            clip_on_vector(3, second_3[b])
+        for b in range(blocks):
+            cols = slice(b * P, (b + 1) * P)
+            nc.vector.tensor_tensor(planes[:, 1, cols], second_3[b], part_3[:, cols], ALU.add)
+        for b in range(blocks):
+            cols = slice(b * P, (b + 1) * P)
+            nc.vector.tensor_copy(grouped[1][:, cols, 2:], planes[:, :, cols].rearrange("p e n -> p n e"))
+        last_layer(HALF, P, (nc.scalar.copy,))
+        last_layer(HALF + P, P, (nc.scalar.copy, nc.vector.tensor_copy))

from contextlib import ExitStack

import concourse.mybir as mybir
from concourse.masks import make_identity

K, T, S, N, H = 512, 2048, 512, 512, 512
FLOPS = 2 * K * H * S * 2 + 2 * H * N * S

F32 = mybir.dt.float32
BF16 = mybir.dt.bfloat16
I32 = mybir.dt.int32
U32 = mybir.dt.uint32
U16 = mybir.dt.uint16
U8 = mybir.dt.uint8
FP8X4 = mybir.dt.float8_e4m3fn_x4
ALU = mybir.AluOpType
ACT = mybir.ActivationFunctionType

P = 128
PACK = 4
CLIP = 0.75
HALF = S // 2
WIDE = 2 * S
LIST_COLS = S // 16


def tile_picked_bpclip_none_p_kernel(
    tc, x_words, x_scales, w1, w2, gn, w3, offs, p1, r1, p2, r2, out
):
    nc = tc.nc
    with ExitStack() as ctx:
        keep = ctx.enter_context(tc.tile_pool(name="keep", bufs=1))
        ring = ctx.enter_context(tc.tile_pool(name="ring", bufs=4))
        pair = ctx.enter_context(tc.tile_pool(name="pair", bufs=2))
        psum = ctx.enter_context(tc.psum_pool(name="psum", bufs=4))
        psum_turn = ctx.enter_context(tc.psum_pool(name="psum_turn", bufs=2))

        def load_list(src, name):
            tile = keep.tile([P, LIST_COLS], U16, name=name)
            nc.sync.dma_start(tile[:], src)
            return tile

        def load_rows(w, name, pieces=1):
            raw = keep.tile([P, PACK, w.shape[1]], F32, name=name)
            rows = w.rearrange("(p j) c -> p j c", j=PACK)
            step = PACK // pieces
            for j in range(0, PACK, step):
                nc.sync.dma_start(raw[:, j : j + step, :], rows[:, j : j + step, :])
            return raw

        def quantize(grouped, width, pool, name):
            codes = pool.tile([P, width], U32, name=name + "_codes", align_bytes=64)
            scales = pool.tile([P, width], U8, name=name + "_scales", align_bytes=64)
            nc.vector.quantize_mx(out=codes[:].bitcast(FP8X4), scales=scales[:], in_=grouped)
            return codes, scales

        def deal_columns(raw, u, tag, copy):
            grouped = keep.tile([P, 2 * P * PACK], BF16, name="dealt", tag=tag, align_bytes=64)
            copy(
                grouped[:].rearrange("p (e m j) -> p m j e", e=2, j=PACK),
                raw[:].rearrange("p j (m t) -> p m j t", t=PACK)[:, :, :, 2 * u : 2 * u + 2],
            )
            return grouped[:]

        def product(acc, lhs, cols, rhs, rhs_cols=slice(None)):
            nc.tensor.matmul_mx(
                out=acc,
                lhsT=lhs[0][:, cols].bitcast(FP8X4),
                lhsT_scale=lhs[1][:, cols],
                rhs=rhs[0][:, rhs_cols].bitcast(FP8X4),
                rhs_scale=rhs[1][:, rhs_cols],
                start=True,
                stop=True,
            )

        scale_table = keep.tile([P, T], U8, name="scale_table", tag="w1_0_codes", align_bytes=64)
        nc.vector.memset(scale_table[:].bitcast(I32), 0)
        gain = keep.tile([P, PACK], F32, name="gain")
        nc.sync.dma_start(gain[:], gn.rearrange("(p t) o -> p (t o)", t=PACK))
        offs_t = load_list(offs, "offs_t")
        w1_raw = load_rows(w1, "w1_raw")
        for q in range(4):
            nc.sync.dma_start(
                scale_table[32 * q : 32 * q + 4, :].bitcast(I32),
                x_scales[0, 4 * q : 4 * q + 4, :].bitcast(I32),
            )
        word_table = keep.tile([P, T], U32, name="word_table", tag="w1_dealt_1", align_bytes=64)
        nc.sync.dma_start(
            word_table[:].bitcast(I32), x_words[0].rearrange("p c r -> p (c r)").bitcast(I32)
        )
        w2_raw = load_rows(w2, "w2_raw")
        p_lists = [load_list(p1, "p1_t"), load_list(p2, "p2_t")]
        r_lists = [load_list(r1, "r1_t"), load_list(r2, "r2_t")]
        w3_raw = load_rows(w3, "w3_raw")

        identity = keep.tile([P, P], F32, name="identity")
        make_identity(nc, identity[:])

        def window(name, width):
            rows = keep.tile([P, width], F32, name=name, align_bytes=64)
            if width > S:
                nc.vector.memset(rows[:, S:], 0.0)
            return rows

        beliefs = [window(f"belief_{t}", WIDE) for t in range(PACK)]
        messages = [window(f"message_{t}", WIDE if t == 0 else S) for t in range(PACK)]

        def column_table(name, source, func, scale):
            table = keep.tile([P, PACK], F32, name=name)
            nc.scalar.activation(table[:], source[:], func, scale=scale)
            return table

        span = column_table("span", gain, ACT.Abs, 2 * CLIP)
        lift = column_table("lift", gain, ACT.Abs, 3 * CLIP)
        neg_span = column_table("neg_span", span, ACT.Copy, -1.0)
        neg_gain = column_table("neg_gain", gain, ACT.Copy, -1.0)

        x_scale = keep.tile([P, S], U8, name="x_scale", align_bytes=64)
        nc.vector.tensor_copy(x_scale[:], scale_table[:].indirect(offs_t[:]))
        w1_q = [quantize(deal_columns(w1_raw, 0, "w1_dealt_0", nc.scalar.copy), 2 * P, keep, "w1_0")]
        x_code = keep.tile([P, S], U32, name="x_code", align_bytes=64)
        for half in range(2):
            nc.vector.tensor_copy(
                x_code[:, half * S // 2 : (half + 1) * S // 2],
                word_table[:].indirect(offs_t[:, half * LIST_COLS // 2 : (half + 1) * LIST_COLS // 2]),
            )
        x_q = (x_code, x_scale)
        w1_q.append(quantize(deal_columns(w1_raw, 1, "w1_dealt_1", nc.vector.tensor_copy), 2 * P, keep, "w1_1"))

        def first_layer(w_q, t, rows, scale, bias, pieces=1):
            u, e = divmod(t, 2)
            width = S // pieces
            for lo in range(0, S, width):
                acc = psum.tile([P, width], F32, name="acc")
                product(acc[:], w_q[u], slice(e * P, (e + 1) * P), x_q, slice(lo, lo + width))
                nc.scalar.activation(
                    rows[t][:, lo : lo + width], acc[:], ACT.Identity, bias=bias[:, t : t + 1], scale=scale[:, t : t + 1]
                )

        fetched = {}

        def fetch_beliefs(t, tag):
            fetched[t] = keep.tile([P, 2, S], F32, name=f"fetched_{t}", tag=tag, align_bytes=64)
            for d in range(2):
                nc.vector.tensor_copy(fetched[t][:, d, :], beliefs[t][:].indirect(p_lists[d][:]))

        first_layer(w1_q, 0, beliefs, gain, neg_span, pieces=2)
        first_layer(w1_q, 1, beliefs, gain, neg_span)
        fetch_beliefs(0, "fetched_0")
        w2_q = [quantize(deal_columns(w2_raw, 0, "fetched_1", nc.scalar.copy), 2 * P, keep, "w2_0")]
        fetch_beliefs(1, "fetched_1")
        for t in range(2):
            first_layer(w2_q, t, messages, neg_gain, lift)
        w2_q.append(quantize(deal_columns(w2_raw, 1, "w2_dealt_1", nc.scalar.copy), 2 * P, keep, "w2_1"))
        for t in range(2, PACK):
            first_layer(w1_q, t, beliefs, gain, neg_span)
        for t in range(2, PACK):
            first_layer(w2_q, t, messages, neg_gain, lift)

        w3_grouped = keep.tile([P, PACK * N], BF16, name="w3_grouped", align_bytes=64)
        nc.scalar.copy(
            w3_grouped[:].rearrange("p (c i j) -> p c j i", i=4, j=PACK),
            w3_raw[:].rearrange("p j (c i) -> p c j i", i=4),
        )
        w3_q = quantize(w3_grouped[:], N, keep, "w3")

        def difference(dst, t, d, lo, width):
            picks = r_lists[d][:, lo // 16 : (lo + width) // 16]
            nc.vector.tensor_tensor(dst, messages[t][:].indirect(picks), fetched[t][:, d, lo : lo + width], ALU.add)

        def differences(t, lo, width):
            terms = ring.tile([P, 2, width], F32, name="terms")
            for d in range(2):
                difference(terms[:, d, :], t, d, lo, width)
            return terms

        def clip_on_vector(t, flat):
            nc.vector.tensor_scalar(flat, flat, 0.0, span[:, t : t + 1], ALU.max, ALU.min)

        def clip_on_scalar(t, flat):
            for step in range(2):
                nc.scalar.activation(flat, flat, ACT.Relu, bias=span[:, t : t + 1], scale=-1.0)

        blocks = HALF // P
        sums, words = {}, {}
        grouped = [keep.tile([P, HALF, PACK], BF16, name=f"z_grouped_{h}", align_bytes=64) for h in range(2)]
        planes = keep.tile([P, 2, HALF], BF16, name="planes")

        def add_turned(t, h, terms, terms_lo):
            u, e = divmod(t, 2)
            if e == 0:
                sums[h, u] = psum_turn.tile([P, blocks, 2, P], F32, name="turned_sum")
            for b in range(blocks):
                tok = h * HALF + b * P
                parts = [beliefs[t][:, tok : tok + P]]
                parts += [terms[:, d, tok - terms_lo : tok - terms_lo + P] for d in range(2)]
                for i, part in enumerate(parts):
                    nc.tensor.matmul(
                        sums[h, u][:, b, e, :], part, identity[:], start=(i == 0), stop=(i == 2), is_transpose=True
                    )

        def turn_back(h, u):
            z_rows = pair.tile([P, blocks, P, 2], BF16, name="z_rows")
            nc.scalar.copy(z_rows[:], sums[h, u][:].rearrange("n b e p -> n b p e"))
            if u == 0:
                words[h] = psum_turn.tile([P, blocks, 2, P], F32, name="words")
            z_words = z_rows[:].rearrange("n b p e -> n (b p e)").bitcast(F32)
            for b in range(blocks):
                nc.tensor.transpose(words[h][:, b, u, :], z_words[:, b * P : (b + 1) * P], identity[:])

        def group_words(h, pairs):
            dst = grouped[h][:].bitcast(F32).rearrange("p (b n) u -> p b n u", n=P)
            nc.scalar.copy(dst[:, :, :, :pairs], words[h][:].rearrange("p b u n -> p b n u")[:, :, :, :pairs])

        def last_layer(lo, width, copies):
            h, first = divmod(lo, HALF)
            z_q = quantize(grouped[h][:, first : first + width, :].rearrange("p n t -> p (n t)"), width, pair, "z")
            tiles = PACK // len(copies)
            for i, copy in enumerate(copies):
                acc = psum.tile([P, tiles, width], F32, name="acc")
                for j in range(tiles):
                    m = tiles * i + j
                    product(acc[:, j, :], w3_q, slice(m * P, (m + 1) * P), z_q)
                result = keep.tile([P, tiles, width], F32, name=f"result_{lo}_{i}")
                copy(result[:], acc[:])
                rows = out[i * tiles * P : (i + 1) * tiles * P, lo : lo + width]
                nc.sync.dma_start(rows.rearrange("(j p) n -> p j n", p=P), result[:])

        def finish(t, lo, width, terms):
            clip = clip_on_vector if t == PACK - 1 else clip_on_scalar
            clip(t, terms[:].rearrange("p d n -> p (d n)"))
            for h in range(lo // HALF, (lo + width) // HALF):
                add_turned(t, h, terms, lo)
                if t % 2 == 1:
                    turn_back(h, t // 2)

        terms_0 = differences(0, 0, S)
        terms_1 = differences(1, 0, HALF)
        fetch_beliefs(2, "fetched_0")
        finish(0, 0, S, terms_0)
        terms_2 = differences(2, 0, HALF)
        fetch_beliefs(3, "message_0")
        finish(1, 0, HALF, terms_1)
        terms_3 = differences(3, 0, HALF)
        finish(2, 0, HALF, terms_2)
        finish(3, 0, HALF, terms_3)
        group_words(0, 2)
        last_layer(0, HALF, (nc.scalar.copy, nc.scalar.copy))

        terms_1 = differences(1, HALF, HALF)
        terms_2 = differences(2, HALF, HALF)
        finish(1, HALF, HALF, terms_1)
        group_words(1, 1)

        early_3 = ring.tile([P, HALF + P], F32, name="terms")
        last_3 = keep.tile([P, P], F32, name="last_3", tag="z_grouped_0", align_bytes=64)
        first_3, second_3 = early_3[:, :HALF], (early_3[:, HALF:], last_3[:])
        part_2 = keep.tile([P, HALF], F32, name="part_2")
        part_3 = keep.tile([P, HALF], F32, name="part_3")
        difference(first_3, 3, 0, HALF, HALF)
        clip_on_vector(2, terms_2[:].rearrange("p d n -> p (d n)"))
        difference(second_3[0], 3, 1, HALF, P)
        nc.vector.tensor_tensor(part_2[:], terms_2[:, 0, :], beliefs[2][:, HALF:S], ALU.add)
        clip_on_vector(3, first_3)
        nc.vector.tensor_tensor(planes[:, 0, :], terms_2[:, 1, :], part_2[:], ALU.add)
        difference(second_3[1], 3, 1, HALF + P, P)
        nc.vector.tensor_tensor(part_3[:], first_3, beliefs[3][:, HALF:S], ALU.add)
        for b in range(blocks):
            clip_on_vector(3, second_3[b])
        for b in range(blocks):
            cols = slice(b * P, (b + 1) * P)
            nc.vector.tensor_tensor(planes[:, 1, cols], second_3[b], part_3[:, cols], ALU.add)
        for b in range(blocks):
            cols = slice(b * P, (b + 1) * P)
            nc.vector.tensor_copy(grouped[1][:, cols, 2:], planes[:, :, cols].rearrange("p e n -> p n e"))
        last_layer(HALF, P, (nc.scalar.copy,))
        last_layer(HALF + P, P, (nc.scalar.copy, nc.vector.tensor_copy))
